import numpy as np
import ml_dtypes


def mxq(x, axis, fmt="e4m3"):
    dtype, down = {"e4m3": (ml_dtypes.float8_e4m3fn, 7), "e5m2": (ml_dtypes.float8_e5m2, 14)}[fmt]
    v = np.moveaxis(np.asarray(x, np.float32).astype(ml_dtypes.bfloat16).astype(np.float64), axis, -1)
    blocks = v.reshape(v.shape[:-1] + (-1, 32))
    amax = np.abs(blocks).max(-1, keepdims=True)
    byte = np.maximum(np.where(amax > 0, np.frexp(amax)[1] - 1 + 127, 0) - down, 1)
    scale = np.exp2(byte - 127.0)
    codes = (blocks / scale).astype(np.float32).astype(dtype).astype(np.float64)
    return np.moveaxis((codes * scale).reshape(v.shape), -1, axis)


WIDE = False


def mx_kscale(k):
    if not WIDE:
        return np.ones(k)
    levels = np.array([10, -10, 5, -5, 0])
    if k % 512:
        return np.exp2(np.random.permutation(np.resize(levels, k // 32))).repeat(32)
    a = np.empty((k // 512, 16))
    for p in range(k // 512):
        a[p, :8] = np.random.permutation(np.resize(levels, 8))
        for g in range(8):
            far = levels[np.abs(levels - a[p, g]) >= 10]
            a[p, g + 8] = far[np.random.randint(len(far))]
    return np.exp2(a.ravel()).repeat(32)


def f64(x):
    return np.asarray(x).astype(np.float64)


def striped(idx):
    return np.tile(idx.reshape(-1, 16).T, (8, 1)).astype(np.uint16)


def unstriped(offs):
    return offs[:16].T.reshape(-1).astype(np.int64)


E2M1 = np.array([0.0, 0.5, 1.0, 1.5, 2.0, 3.0, 4.0, 6.0, -0.0, -0.5, -1.0, -1.5, -2.0, -3.0, -4.0, -6.0])


def pack_weight(w, fmt):
    k, n = w.shape
    w = f64(np.asarray(w, np.float32).astype(ml_dtypes.bfloat16)).reshape(k // 32, 32, n)
    amax = np.abs(w).max(1)
    if fmt == "e4m3":
        byte = np.frexp(amax)[1] - 1 + 127 - 7
    else:
        mant, ex = np.frexp(amax / 6.0)
        byte = np.where(mant > 0.5, ex, ex - 1) + 127
    byte = np.clip(np.where(amax > 0, byte, 1), 1, 254)
    scaled = (w * np.exp2(127.0 - byte)[:, None, :]).reshape(k, n).astype(np.float32)
    by_word = np.ascontiguousarray(scaled.reshape(k // 512, 128, 4, n).transpose(0, 1, 3, 2))
    if fmt == "e4m3":
        words = by_word.astype(ml_dtypes.float8_e4m3fn).view(np.uint8)
    else:
        c = by_word.astype(ml_dtypes.float4_e2m1fn).view(np.uint8) & 0xF
        words = (c[..., 0::2] | (c[..., 1::2] << 4)).reshape(k // 512, 128, 2 * n)
    return np.ascontiguousarray(words), np.ascontiguousarray(byte.astype(np.uint8).reshape(k // 512, 16, n))


def unpack_weight(words, scales, fmt):
    g, _, n = scales.shape
    words = np.ascontiguousarray(words).reshape(g, 128, n, -1)
    if fmt == "e4m3":
        vals = words.view(ml_dtypes.float8_e4m3fn).astype(np.float64)
    else:
        nib = np.empty((g, 128, n, 4), np.uint8)
        nib[..., 0::2] = words & 0xF
        nib[..., 1::2] = words >> 4
        vals = E2M1[nib]
    vals = vals * np.repeat(np.exp2(scales.astype(np.float64) - 127.0), 8, axis=1)[..., None]
    return vals.transpose(0, 1, 3, 2).reshape(g * 512, n)


def gelu(v):
    return 0.5 * v * (1.0 + np.tanh(np.sqrt(2.0 / np.pi) * (v + 0.044715 * v**3)))


K, K2, T, S, H, N = 1024, 1536, 4096, 1024, 512, 384

def setup_inputs():
    n = np.random.standard_normal
    s = mx_kscale(K)[:, None]
    s2 = mx_kscale(K2)[:, None]
    u = mx_kscale(H)[:, None]
    d = {}
    d["tab_words"], d["tab_scales"] = pack_weight(n((K, T)) * s, "e4m3")
    d["offs"] = striped(np.random.permutation(T)[:S])
    d["xs_words"], d["xs_scales"] = pack_weight(n((K2, S)) * s2, "e4m3")
    d["w1"] = (n((K, H)) / s * u.T / K**0.5).astype(np.float32)
    d["w2_words"], d["w2_scales"] = pack_weight(n((K, H)) / s * u.T / K**0.5, "e2m1")
    d["w3"] = (n((K2, H)) / s2 * u.T / K2**0.5).astype(np.float32)
    d["w4_words"], d["w4_scales"] = pack_weight(n((H, N)) / u / H**0.5, "e4m3")
    d["tol"] = np.random.uniform(0.5, 1.5, N).astype(np.float32)
    return d

def reference(tab_words, tab_scales, offs, xs_words, xs_scales, w1, w2_words, w2_scales, w3, w4_words, w4_scales, tol):
    v = unpack_weight(tab_words, tab_scales, "e4m3")[:, unstriped(offs)]
    xs = unpack_weight(xs_words, xs_scales, "e4m3")
    w2 = unpack_weight(w2_words, w2_scales, "e2m1")
    w4 = unpack_weight(w4_words, w4_scales, "e4m3")
    y1 = mxq(f64(w1), 0, "e4m3").T @ v
    y2 = w2.T @ v
    y3 = mxq(f64(w3), 0, "e4m3").T @ xs
    hi = np.maximum(np.maximum(y1, y2), y3)
    lo = np.minimum(np.minimum(y1, y2), y3)
    h = hi - lo
    y = w4.T @ mxq(h, 0, "e4m3")
    return y - f64(tol)[:, None]

@@ -1,0 +1,267 @@
+from contextlib import ExitStack
+
+import concourse.mybir as mybir
+
+K, K2, T, S, H, N = 1024, 1536, 4096, 1024, 512, 384
+FLOPS = 2 * S * (2 * K * H + K2 * H + H * N)
+
+F32 = mybir.dt.float32
+BF16 = mybir.dt.bfloat16
+I32 = mybir.dt.int32
+U32 = mybir.dt.uint32
+U16 = mybir.dt.uint16
+U8 = mybir.dt.uint8
+FP8X4 = mybir.dt.float8_e4m3fn_x4
+FP4X4 = mybir.dt.float4_e2m1fn_x4
+ALU = mybir.AluOpType
+ACT = mybir.ActivationFunctionType
+
+P = 128
+PACK = 4
+KP = P * PACK
+TOK = 128
+NT = S // TOK
+PA, PB = K // KP, K2 // KP
+NB = N // P
+HALF = S // 2
+XS_TOK = 256
+STORE_GROUPS = ((0, 1), (2, 3), (4, 5), (6,), (7,))
+GPSIMD_TILES = NT - 1
+
+
+def tile_list_dyelot_spread_check_kernel(
+    tc, tab_words, tab_scales, offs, xs_words, xs_scales, w1, w2_words, w2_scales, w3, w4_words, w4_scales, tol, out
+):
+    nc = tc.nc
+    with ExitStack() as ctx:
+        keep = ctx.enter_context(tc.tile_pool(name="keep", bufs=1))
+        ring = ctx.enter_context(tc.tile_pool(name="ring", bufs=3))
+        ypsum = ctx.enter_context(tc.psum_pool(name="ypsum", bufs=6))
+        opsum = ctx.enter_context(tc.psum_pool(name="opsum", bufs=2))
+
+        def held(shape, dtype, name, tag=""):
+            return keep.tile(shape, dtype, name=name, tag=tag or name, align_bytes=64)
+
+        offsets = keep.tile([P, S // 16], U16, name="offsets")
+        nc.sync.dma_start(offsets[:], offs)
+
+        tol_sb = held([P, NB], F32, "tol_sb")
+        neg_tol = held([P, NB], F32, "neg_tol")
+        with nc.allow_non_contiguous_dma(reason="one tolerance to a partition"):
+            nc.scalar.dma_start(out=tol_sb[:], in_=tol.rearrange("(b p) -> p b", p=P))
+        nc.scalar.mul(neg_tol[:], tol_sb[:], -1.0)
+
+        tab_sc = held([P, T], U8, "tab_sc")
+        nc.vector.memset(tab_sc[:].bitcast(I32), 0)
+        w2_sc_raw = held([P, PA, H], U8, "w2_sc_raw")
+        v_sc1 = held([P, S], U8, "v_sc1")
+        xs_sc = held([P, PB, S], U8, "xs_sc")
+        w4_sc = held([P, N], U8, "w4_sc")
+        for plane in (w2_sc_raw, v_sc1, xs_sc, w4_sc):
+            nc.gpsimd.memset(plane[:].bitcast(I32), 0)
+
+        for q in range(4):
+            nc.scalar.dma_start(
+                out=tab_sc[32 * q : 32 * q + 4 * PA, :].bitcast(I32),
+                in_=tab_scales[:, 4 * q : 4 * q + 4, :].bitcast(I32),
+            )
+
+        def load_table(a):
+            words = held([P, T], I32, f"tab{a}")
+            nc.sync.dma_start(out=words[:], in_=tab_words[a].rearrange("p t i -> p (t i)").bitcast(I32))
+            return words
+
+        tab0 = load_table(0)
+        w2_raw = held([P, PA, 2 * H], U8, "w2_raw")
+        nc.sync.dma_start(out=w2_raw[:].bitcast(I32), in_=w2_words.rearrange("a p c -> p a c").bitcast(I32))
+        for q in range(4):
+            nc.sync.dma_start(
+                out=w2_sc_raw[32 * q : 32 * q + 4, :, :].bitcast(I32),
+                in_=w2_scales[:, 4 * q : 4 * q + 4, :].rearrange("a r c -> r a c").bitcast(I32),
+            )
+        tab1 = load_table(1)
+
+        def load_weight(w, a, c0, c1, name):
+            raw = held([P, PACK, c1 - c0], F32, name)
+            rows = w[a * KP : (a + 1) * KP, c0:c1]
+            nc.sync.dma_start(out=raw[:], in_=rows.rearrange("(p j) c -> p j c", j=PACK))
+            return raw
+
+        w1_raw0 = load_weight(w1, 0, 0, H, "w1_raw0")
+        w1_raw1 = [load_weight(w1, 1, c, c + H // 2, f"w1_raw1_{c}") for c in (0, H // 2)]
+
+        v_sc = held([P, S], U8, "v_sc")
+        nc.vector.tensor_copy(v_sc[:], tab_sc[:].indirect(offsets[:]))
+        for q in range(4):
+            nc.scalar.dma_start(
+                out=v_sc1[32 * q : 32 * q + 4, :].bitcast(I32),
+                in_=v_sc[32 * q + 4 : 32 * q + 8, :].bitcast(I32),
+            )
+
+        w3_raw = [load_weight(w3, a, 0, H, f"w3_raw{a}") for a in range(PB)]
+        for q in range(4):
+            nc.sync.dma_start(
+                out=xs_sc[32 * q : 32 * q + 4, :, :].bitcast(I32),
+                in_=xs_scales[:, 4 * q : 4 * q + 4, :].rearrange("a r c -> r a c").bitcast(I32),
+            )
+        xs = []
+        for g in range(S // XS_TOK):
+            part = held([P, PB, XS_TOK], I32, f"xs{g}")
+            cols = xs_words[:, :, g * XS_TOK : (g + 1) * XS_TOK, :]
+            nc.sync.dma_start(out=part[:], in_=cols.rearrange("a p c i -> p a (c i)").bitcast(I32))
+            xs.append(part)
+        w4 = held([P, N], I32, "w4")
+        nc.sync.dma_start(out=w4[:], in_=w4_words[0].rearrange("p c i -> p (c i)").bitcast(I32))
+        for q in range(4):
+            nc.sync.dma_start(
+                out=w4_sc[32 * q : 32 * q + 4, :].bitcast(I32),
+                in_=w4_scales[0, 4 * q : 4 * q + 4, :].bitcast(I32),
+            )
+
+        v0 = held([P, S], U32, "v0")
+        nc.vector.tensor_copy(v0[:], tab0[:].bitcast(U32).indirect(offsets[:]))
+
+        w2 = held([P, PA, 2 * H], U8, "w2")
+        nc.vector.tensor_copy(
+            out=w2[:].bitcast(U16).rearrange("p a (t m) -> p a t m", t=PACK),
+            in_=w2_raw[:].bitcast(U16).rearrange("p a (m t) -> p a t m", t=PACK),
+        )
+        w2_sc = held([P, PA, H], U8, "w2_sc")
+        nc.vector.tensor_copy(
+            out=w2_sc[:].rearrange("p a (t m) -> p a t m", t=PACK),
+            in_=w2_sc_raw[:].rearrange("p a (m t) -> p a t m", t=PACK),
+        )
+
+        v1 = []
+        for g in range(2):
+            part = held([P, HALF], U32, f"v1_{g}")
+            lst = offsets[:, g * (HALF // 16) : (g + 1) * (HALF // 16)]
+            nc.vector.tensor_copy(part[:], tab1[:].bitcast(U32).indirect(lst))
+            v1.append(part)
+
+        def v_operand(a, i):
+            cols = slice(i * TOK, (i + 1) * TOK)
+            if a == 0:
+                return v0[:, cols].bitcast(FP8X4), v_sc[:, cols]
+            g, c = divmod(i * TOK, HALF)
+            return v1[g][:, c : c + TOK].bitcast(FP8X4), v_sc1[:, cols]
+
+        def xs_operand(a, i):
+            g, c = divmod(i * TOK, XS_TOK)
+            return xs[g][:, a, c : c + TOK].bitcast(FP8X4), xs_sc[:, a, i * TOK : (i + 1) * TOK]
+
+        def w2_operand(a, t):
+            return w2[:, a, 2 * P * t : 2 * P * (t + 1)].bitcast(FP4X4), w2_sc[:, a, P * t : P * (t + 1)]
+
+        def round_weight(copy, raw, grouped, m0):
+            width = raw.shape[2] // PACK
+            dst = grouped[:].rearrange("p (t m j) -> p m j t", t=PACK, j=PACK)[:, m0 : m0 + width, :, :]
+            copy(out=dst, in_=raw[:].rearrange("p j (m t) -> p m j t", t=PACK))
+
+        def quantise_weight(grouped, name, tag=""):
+            codes = held([P, H], U32, name + "_codes", tag)
+            scales = held([P, H], U8, name + "_scales")
+            nc.vector.quantize_mx(out=codes[:].bitcast(FP8X4), scales=scales[:], in_=grouped[:])
+            return codes, scales
+
+        def weight_operand(quantised):
+            def operand(a, t):
+                codes, scales = quantised[a]
+                return codes[:, P * t : P * (t + 1)].bitcast(FP8X4), scales[:, P * t : P * (t + 1)]
+
+            return operand
+
+        def product(weight, moving, passes, i):
+            bank = ypsum.tile([P, PACK, TOK], F32, name="ybank")
+            for t in range(PACK):
+                for a in range(passes):
+                    lhsT, lhsT_scale = weight(a, t)
+                    rhs, rhs_scale = moving(a, i)
+                    nc.tensor.matmul_mx(
+                        out=bank[:, t, :], lhsT=lhsT, lhsT_scale=lhsT_scale, rhs=rhs, rhs_scale=rhs_scale,
+                        start=(a == 0), stop=(a == passes - 1),
+                    )
+            return bank[:].rearrange("p t n -> p n t")
+
+        def by_token(tile):
+            return tile[:].rearrange("p (n t) -> p n t", t=PACK)
+
+        y2 = []
+        for i in range(NT):
+            y2_sb = held([P, KP], F32, f"y2_{i}")
+            nc.scalar.copy(out=by_token(y2_sb), in_=product(w2_operand, v_operand, PA, i))
+            y2.append(y2_sb)
+
+        w1_q = []
+        grouped = held([P, PACK * H], BF16, "w1_grouped0")
+        round_weight(nc.vector.tensor_copy, w1_raw0, grouped, 0)
+        w1_q.append(quantise_weight(grouped, "w1_0"))
+        grouped = held([P, PACK * H], BF16, "w1_grouped1")
+        for g in range(2):
+            round_weight(nc.vector.tensor_copy, w1_raw1[g], grouped, g * P // 2)
+        w1_q.append(quantise_weight(grouped, "w1_1"))
+
+        w3_grouped = []
+        for a in range(PB):
+            grouped = held([P, PACK * H], BF16, f"w3_grouped{a}")
+            round_weight(nc.scalar.copy, w3_raw[a], grouped, 0)
+            w3_grouped.append(grouped)
+
+        hi12, lo12, w3_q = [], [], []
+        for i in range(NT):
+            y1 = product(weight_operand(w1_q), v_operand, PA, i)
+            hi = held([P, KP], F32, f"hi12_{i}")
+            lo = held([P, KP], F32, f"lo12_{i}")
+            nc.vector.tensor_tensor(out=by_token(hi), in0=y1, in1=by_token(y2[i]), op=ALU.max)
+            nc.vector.tensor_tensor(out=by_token(lo), in0=y1, in1=by_token(y2[i]), op=ALU.min)
+            hi12.append(hi)
+            lo12.append(lo)
+            if i in (2, 4, 6):
+                a = len(w3_q)
+                w3_q.append(quantise_weight(w3_grouped[a], f"w3_{a}", f"y2_{i}"))
+
+        out_rows = out.rearrange("(b p) j -> p b j", p=P)
+        staged = {}
+        for group in STORE_GROUPS:
+            tile = held([P, NB, len(group) * TOK], F32, f"staged{group[0]}")
+            for i in group:
+                staged[i] = (tile, group)
+
+        def spread(i):
+            y3 = product(weight_operand(w3_q), xs_operand, PB, i)
+            hi = ring.tile([P, KP], F32, name="hi")
+            lo = ring.tile([P, KP], F32, name="lo")
+            nc.vector.tensor_tensor(out=by_token(hi), in0=y3, in1=by_token(hi12[i]), op=ALU.max)
+            nc.vector.tensor_tensor(out=by_token(lo), in0=y3, in1=by_token(lo12[i]), op=ALU.min)
+            h = ring.tile([P, KP], BF16, name="h", align_bytes=64)
+            engine = nc.gpsimd if i < GPSIMD_TILES else nc.vector
+            engine.tensor_tensor(out=h[:], in0=hi[:], in1=lo[:], op=ALU.subtract)
+            return h
+
+        def score(i, h):
+            codes = ring.tile([P, TOK], U32, name="h_codes", align_bytes=64)
+            scales = ring.tile([P, TOK], U8, name="h_scales", align_bytes=64)
+            nc.vector.quantize_mx(out=codes[:].bitcast(FP8X4), scales=scales[:], in_=h[:])
+            bank = opsum.tile([P, NB, TOK], F32, name="obank")
+            for b in range(NB):
+                nc.tensor.matmul_mx(
+                    out=bank[:, b, :], lhsT=w4[:, P * b : P * (b + 1)].bitcast(FP8X4),
+                    lhsT_scale=w4_sc[:, P * b : P * (b + 1)], rhs=codes[:].bitcast(FP8X4), rhs_scale=scales[:],
+                    start=True, stop=True,
+                )
+            tile, group = staged[i]
+            c = (i - group[0]) * TOK
+            for b in range(NB):
+                nc.scalar.activation(
+                    out=tile[:, b, c : c + TOK], in_=bank[:, b, :], func=ACT.Identity, bias=neg_tol[:, b : b + 1]
+                )
+            if i == group[-1]:
+                nc.sync.dma_start(out=out_rows[:, :, group[0] * TOK : (i + 1) * TOK], in_=tile[:])
+
+        pending = None
+        for i in range(NT):
+            h = spread(i)
+            if pending is not None:
+                score(i - 1, pending)
+            pending = h
+        score(NT - 1, pending)

@@ -26,7 +26,8 @@ NB = N // P
 HALF = S // 2
 XS_TOK = 256
 STORE_GROUPS = ((0, 1), (2, 3), (4, 5), (6,), (7,))
-GPSIMD_TILES = NT - 1
+GPSIMD_TILES = 0
+Y_BANKS = 6
 
 
 def tile_list_dyelot_spread_check_kernel(
@@ -36,7 +37,7 @@ def tile_list_dyelot_spread_check_kernel(
     with ExitStack() as ctx:
         keep = ctx.enter_context(tc.tile_pool(name="keep", bufs=1))
         ring = ctx.enter_context(tc.tile_pool(name="ring", bufs=3))
-        ypsum = ctx.enter_context(tc.psum_pool(name="ypsum", bufs=6))
+        ypsum = ctx.enter_context(tc.psum_pool(name="ypsum", bufs=Y_BANKS))
         opsum = ctx.enter_context(tc.psum_pool(name="opsum", bufs=2))
 
         def held(shape, dtype, name, tag=""):
@@ -187,10 +188,19 @@ def tile_list_dyelot_spread_check_kernel(
             return tile[:].rearrange("p (n t) -> p n t", t=PACK)
 
         y2 = []
-        for i in range(NT):
+
+        def second_reading(i):
             y2_sb = held([P, KP], F32, f"y2_{i}")
             nc.scalar.copy(out=by_token(y2_sb), in_=product(w2_operand, v_operand, PA, i))
             y2.append(y2_sb)
+
+        def round_w3(a):
+            grouped = held([P, PACK * H], BF16, f"w3_grouped{a}")
+            round_weight(nc.scalar.copy, w3_raw[a], grouped, 0)
+            return grouped
+
+        for i in range(Y_BANKS):
+            second_reading(i)
 
         w1_q = []
         grouped = held([P, PACK * H], BF16, "w1_grouped0")
@@ -201,13 +211,7 @@ def tile_list_dyelot_spread_check_kernel(
             round_weight(nc.vector.tensor_copy, w1_raw1[g], grouped, g * P // 2)
         w1_q.append(quantise_weight(grouped, "w1_1"))
 
-        w3_grouped = []
-        for a in range(PB):
-            grouped = held([P, PACK * H], BF16, f"w3_grouped{a}")
-            round_weight(nc.scalar.copy, w3_raw[a], grouped, 0)
-            w3_grouped.append(grouped)
-
-        hi12, lo12, w3_q = [], [], []
+        hi12, lo12, w3_grouped, w3_q = [], [], [], []
         for i in range(NT):
             y1 = product(weight_operand(w1_q), v_operand, PA, i)
             hi = held([P, KP], F32, f"hi12_{i}")
@@ -216,6 +220,10 @@ def tile_list_dyelot_spread_check_kernel(
             nc.vector.tensor_tensor(out=by_token(lo), in0=y1, in1=by_token(y2[i]), op=ALU.min)
             hi12.append(hi)
             lo12.append(lo)
+            if len(y2) < NT:
+                second_reading(len(y2))
+            if i == 1:
+                w3_grouped = [round_w3(a) for a in range(PB)]
             if i in (2, 4, 6):
                 a = len(w3_q)
                 w3_q.append(quantise_weight(w3_grouped[a], f"w3_{a}", f"y2_{i}"))
@@ -227,12 +235,15 @@ def tile_list_dyelot_spread_check_kernel(
             for i in group:
                 staged[i] = (tile, group)
 
-        def spread(i):
+        def extremes(i):
             y3 = product(weight_operand(w3_q), xs_operand, PB, i)
             hi = ring.tile([P, KP], F32, name="hi")
             lo = ring.tile([P, KP], F32, name="lo")
             nc.vector.tensor_tensor(out=by_token(hi), in0=y3, in1=by_token(hi12[i]), op=ALU.max)
             nc.vector.tensor_tensor(out=by_token(lo), in0=y3, in1=by_token(lo12[i]), op=ALU.min)
+            return hi, lo
+
+        def spread(i, hi, lo):
             h = ring.tile([P, KP], BF16, name="h", align_bytes=64)
             engine = nc.gpsimd if i < GPSIMD_TILES else nc.vector
             engine.tensor_tensor(out=h[:], in0=hi[:], in1=lo[:], op=ALU.subtract)
@@ -260,8 +271,8 @@ def tile_list_dyelot_spread_check_kernel(
 
         pending = None
         for i in range(NT):
-            h = spread(i)
+            hi, lo = extremes(i)
             if pending is not None:
                 score(i - 1, pending)
-            pending = h
+            pending = spread(i, hi, lo)
         score(NT - 1, pending)

@@ -24,10 +24,13 @@ NT = S // TOK
 PA, PB = K // KP, K2 // KP
 NB = N // P
 HALF = S // 2
-XS_TOK = 256
-STORE_GROUPS = ((0, 1), (2, 3), (4, 5), (6,), (7,))
-GPSIMD_TILES = 0
+PAIR = 2 * TOK
+NPAIR = NT // 2
 Y_BANKS = 6
+TAB_HEAD = 1024
+Y2_AHEAD = 2
+W3_ROUND_AFTER = (1, 3, 4)
+W3_QUANT_AFTER = (3, 5, 6)
 
 
 def tile_list_dyelot_spread_check_kernel(
@@ -36,12 +39,29 @@ def tile_list_dyelot_spread_check_kernel(
     nc = tc.nc
     with ExitStack() as ctx:
         keep = ctx.enter_context(tc.tile_pool(name="keep", bufs=1))
-        ring = ctx.enter_context(tc.tile_pool(name="ring", bufs=3))
+        ring = ctx.enter_context(tc.tile_pool(name="ring", bufs=2))
         ypsum = ctx.enter_context(tc.psum_pool(name="ypsum", bufs=Y_BANKS))
         opsum = ctx.enter_context(tc.psum_pool(name="opsum", bufs=2))
 
         def held(shape, dtype, name, tag=""):
             return keep.tile(shape, dtype, name=name, tag=tag or name, align_bytes=64)
+
+        def load_scale_rows(plane, scales):
+            for q in range(4):
+                nc.sync.dma_start(
+                    out=plane[32 * q : 32 * q + 4, :, :].bitcast(I32),
+                    in_=scales[:, 4 * q : 4 * q + 4, :].rearrange("a r c -> r a c").bitcast(I32),
+                )
+
+        def load_rows(raw, w, a, c0, c1):
+            rows = w[a * KP : (a + 1) * KP, c0:c1]
+            nc.sync.dma_start(out=raw, in_=rows.rearrange("(p j) c -> p j c", j=PACK))
+
+        def row_slots(flat):
+            return flat.rearrange("p (j c) -> p j c", j=PACK)
+
+        def table_words(a):
+            return tab_words[a].rearrange("p t i -> p (t i)").bitcast(I32)
 
         offsets = keep.tile([P, S // 16], U16, name="offsets")
         nc.sync.dma_start(offsets[:], offs)
@@ -56,89 +76,104 @@ def tile_list_dyelot_spread_check_kernel(
         nc.vector.memset(tab_sc[:].bitcast(I32), 0)
         w2_sc_raw = held([P, PA, H], U8, "w2_sc_raw")
         v_sc1 = held([P, S], U8, "v_sc1")
-        xs_sc = held([P, PB, S], U8, "xs_sc")
-        w4_sc = held([P, N], U8, "w4_sc")
-        for plane in (w2_sc_raw, v_sc1, xs_sc, w4_sc):
+        for plane in (w2_sc_raw, v_sc1):
             nc.gpsimd.memset(plane[:].bitcast(I32), 0)
 
+        w2_raw = held([P, PA, 2 * H], U8, "w2_raw")
+        nc.sync.dma_start(out=w2_raw[:].bitcast(I32), in_=w2_words.rearrange("a p c -> p a c").bitcast(I32))
+        tab0 = held([P, T], I32, "tab0")
+        nc.sync.dma_start(out=tab0[:, 0:TAB_HEAD], in_=table_words(0)[:, 0:TAB_HEAD])
         for q in range(4):
-            nc.scalar.dma_start(
+            nc.sync.dma_start(
                 out=tab_sc[32 * q : 32 * q + 4 * PA, :].bitcast(I32),
                 in_=tab_scales[:, 4 * q : 4 * q + 4, :].bitcast(I32),
             )
-
-        def load_table(a):
-            words = held([P, T], I32, f"tab{a}")
-            nc.sync.dma_start(out=words[:], in_=tab_words[a].rearrange("p t i -> p (t i)").bitcast(I32))
-            return words
-
-        tab0 = load_table(0)
-        w2_raw = held([P, PA, 2 * H], U8, "w2_raw")
-        nc.sync.dma_start(out=w2_raw[:].bitcast(I32), in_=w2_words.rearrange("a p c -> p a c").bitcast(I32))
-        for q in range(4):
-            nc.sync.dma_start(
-                out=w2_sc_raw[32 * q : 32 * q + 4, :, :].bitcast(I32),
-                in_=w2_scales[:, 4 * q : 4 * q + 4, :].rearrange("a r c -> r a c").bitcast(I32),
-            )
-        tab1 = load_table(1)
-
-        def load_weight(w, a, c0, c1, name):
-            raw = held([P, PACK, c1 - c0], F32, name)
-            rows = w[a * KP : (a + 1) * KP, c0:c1]
-            nc.sync.dma_start(out=raw[:], in_=rows.rearrange("(p j) c -> p j c", j=PACK))
-            return raw
-
-        w1_raw0 = load_weight(w1, 0, 0, H, "w1_raw0")
-        w1_raw1 = [load_weight(w1, 1, c, c + H // 2, f"w1_raw1_{c}") for c in (0, H // 2)]
-
-        v_sc = held([P, S], U8, "v_sc")
-        nc.vector.tensor_copy(v_sc[:], tab_sc[:].indirect(offsets[:]))
-        for q in range(4):
-            nc.scalar.dma_start(
-                out=v_sc1[32 * q : 32 * q + 4, :].bitcast(I32),
-                in_=v_sc[32 * q + 4 : 32 * q + 8, :].bitcast(I32),
-            )
-
-        w3_raw = [load_weight(w3, a, 0, H, f"w3_raw{a}") for a in range(PB)]
-        for q in range(4):
-            nc.sync.dma_start(
-                out=xs_sc[32 * q : 32 * q + 4, :, :].bitcast(I32),
-                in_=xs_scales[:, 4 * q : 4 * q + 4, :].rearrange("a r c -> r a c").bitcast(I32),
-            )
-        xs = []
-        for g in range(S // XS_TOK):
-            part = held([P, PB, XS_TOK], I32, f"xs{g}")
-            cols = xs_words[:, :, g * XS_TOK : (g + 1) * XS_TOK, :]
-            nc.sync.dma_start(out=part[:], in_=cols.rearrange("a p c i -> p a (c i)").bitcast(I32))
-            xs.append(part)
-        w4 = held([P, N], I32, "w4")
-        nc.sync.dma_start(out=w4[:], in_=w4_words[0].rearrange("p c i -> p (c i)").bitcast(I32))
-        for q in range(4):
-            nc.sync.dma_start(
-                out=w4_sc[32 * q : 32 * q + 4, :].bitcast(I32),
-                in_=w4_scales[0, 4 * q : 4 * q + 4, :].bitcast(I32),
-            )
-
-        v0 = held([P, S], U32, "v0")
-        nc.vector.tensor_copy(v0[:], tab0[:].bitcast(U32).indirect(offsets[:]))
+        nc.sync.dma_start(out=tab0[:, TAB_HEAD:T], in_=table_words(0)[:, TAB_HEAD:T])
+        load_scale_rows(w2_sc_raw, w2_scales)
+        w1_raw0 = held([P, PACK * H], F32, "w1_raw0")
+        load_rows(row_slots(w1_raw0[:]), w1, 0, 0, H)
 
         w2 = held([P, PA, 2 * H], U8, "w2")
         nc.vector.tensor_copy(
             out=w2[:].bitcast(U16).rearrange("p a (t m) -> p a t m", t=PACK),
             in_=w2_raw[:].bitcast(U16).rearrange("p a (m t) -> p a t m", t=PACK),
         )
+
+        v_sc = held([P, S], U8, "v_sc")
+        nc.vector.tensor_copy(v_sc[:], tab_sc[:].indirect(offsets[:]))
+        for q in range(4):
+            nc.sync.dma_start(
+                out=v_sc1[32 * q : 32 * q + 4, :].bitcast(I32),
+                in_=v_sc[32 * q + 4 : 32 * q + 8, :].bitcast(I32),
+            )
+        tab1 = held([P, T], I32, "tab1", "tab_sc")
+        nc.sync.dma_start(out=tab1[:], in_=table_words(1))
+
+        v0 = held([P, S], U32, "v0")
+        nc.vector.tensor_copy(v0[:], tab0[:].bitcast(U32).indirect(offsets[:]))
+
         w2_sc = held([P, PA, H], U8, "w2_sc")
         nc.vector.tensor_copy(
             out=w2_sc[:].rearrange("p a (t m) -> p a t m", t=PACK),
             in_=w2_sc_raw[:].rearrange("p a (m t) -> p a t m", t=PACK),
         )
+        w1_raw1 = held([P, PACK * H], F32, "w1_raw1", "w2_sc_raw")
+        w1_halves = []
+        for g in range(2):
+            part = row_slots(w1_raw1[:, g * PACK * H // 2 : (g + 1) * PACK * H // 2])
+            load_rows(part, w1, 1, g * H // 2, (g + 1) * H // 2)
+            w1_halves.append(part)
+
+        def round_weight(copy, raw, grouped, m0):
+            width = raw.shape[2] // PACK
+            dst = grouped[:].rearrange("p (t m j) -> p m j t", t=PACK, j=PACK)[:, m0 : m0 + width, :, :]
+            copy(out=dst, in_=raw.rearrange("p j (m t) -> p m j t", t=PACK))
+
+        def quantise_weight(grouped, name):
+            codes = held([P, H], U32, name + "_codes")
+            scales = held([P, H], U8, name + "_scales")
+            nc.vector.quantize_mx(out=codes[:].bitcast(FP8X4), scales=scales[:], in_=grouped[:])
+            return codes, scales
+
+        grouped = held([P, PACK * H], BF16, "w1_grouped0")
+        round_weight(nc.vector.tensor_copy, row_slots(w1_raw0[:]), grouped, 0)
+        w1_q = [quantise_weight(grouped, "w1_0")]
+
+        w3_all = held([P, PB * PACK * H], F32, "w3_raw", "w1_raw0")
+        w3_raw = []
+        for a in range(PB):
+            part = row_slots(w3_all[:, a * PACK * H : (a + 1) * PACK * H])
+            load_rows(part, w3, a, 0, H)
+            w3_raw.append(part)
+
+        late_sc = held([P, PB * S + N], U8, "late_sc", "w1_grouped0")
+        nc.gpsimd.memset(late_sc[:].bitcast(I32), 0)
+        xs_sc = late_sc[:, 0 : PB * S].rearrange("p (a c) -> p a c", a=PB)
+        w4_sc = late_sc[:, PB * S : PB * S + N]
+        load_scale_rows(xs_sc, xs_scales)
 
         v1 = []
         for g in range(2):
             part = held([P, HALF], U32, f"v1_{g}")
-            lst = offsets[:, g * (HALF // 16) : (g + 1) * (HALF // 16)]
-            nc.vector.tensor_copy(part[:], tab1[:].bitcast(U32).indirect(lst))
+            half_list = offsets[:, g * (HALF // 16) : (g + 1) * (HALF // 16)]
+            nc.vector.tensor_copy(part[:], tab1[:].bitcast(U32).indirect(half_list))
             v1.append(part)
+
+        late_words = held([P, PB * S + N], I32, "late_words", "tab_sc")
+        xs = []
+        for g in range(NPAIR):
+            part = late_words[:, g * PB * PAIR : (g + 1) * PB * PAIR].rearrange("p (a c) -> p a c", a=PB)
+            cols = xs_words[:, :, g * PAIR : (g + 1) * PAIR, :]
+            nc.sync.dma_start(out=part, in_=cols.rearrange("a p c i -> p a (c i)").bitcast(I32))
+            xs.append(part)
+        w4 = late_words[:, PB * S : PB * S + N]
+        nc.sync.dma_start(out=w4, in_=w4_words[0].rearrange("p c i -> p (c i)").bitcast(I32))
+        load_scale_rows(w4_sc.rearrange("p (a c) -> p a c", a=1), w4_scales)
+
+        grouped = held([P, PACK * H], BF16, "w1_grouped1")
+        round_weight(nc.scalar.copy, w1_halves[0], grouped, 0)
+        round_weight(nc.vector.tensor_copy, w1_halves[1], grouped, P // 2)
+        w1_q.append(quantise_weight(grouped, "w1_1"))
 
         def v_operand(a, i):
             cols = slice(i * TOK, (i + 1) * TOK)
@@ -148,22 +183,11 @@ def tile_list_dyelot_spread_check_kernel(
             return v1[g][:, c : c + TOK].bitcast(FP8X4), v_sc1[:, cols]
 
         def xs_operand(a, i):
-            g, c = divmod(i * TOK, XS_TOK)
+            g, c = divmod(i * TOK, PAIR)
             return xs[g][:, a, c : c + TOK].bitcast(FP8X4), xs_sc[:, a, i * TOK : (i + 1) * TOK]
 
         def w2_operand(a, t):
             return w2[:, a, 2 * P * t : 2 * P * (t + 1)].bitcast(FP4X4), w2_sc[:, a, P * t : P * (t + 1)]
-
-        def round_weight(copy, raw, grouped, m0):
-            width = raw.shape[2] // PACK
-            dst = grouped[:].rearrange("p (t m j) -> p m j t", t=PACK, j=PACK)[:, m0 : m0 + width, :, :]
-            copy(out=dst, in_=raw[:].rearrange("p j (m t) -> p m j t", t=PACK))
-
-        def quantise_weight(grouped, name, tag=""):
-            codes = held([P, H], U32, name + "_codes", tag)
-            scales = held([P, H], U8, name + "_scales")
-            nc.vector.quantize_mx(out=codes[:].bitcast(FP8X4), scales=scales[:], in_=grouped[:])
-            return codes, scales
 
         def weight_operand(quantised):
             def operand(a, t):
@@ -184,95 +208,95 @@ def tile_list_dyelot_spread_check_kernel(
                     )
             return bank[:].rearrange("p t n -> p n t")
 
-        def by_token(tile):
-            return tile[:].rearrange("p (n t) -> p n t", t=PACK)
+        def by_token(flat, i):
+            return flat[:, i * KP : (i + 1) * KP].rearrange("p (n t) -> p n t", t=PACK)
 
-        y2 = []
+        y2 = held([P, NT * KP], F32, "y2", "w2_sc_raw")
 
         def second_reading(i):
-            y2_sb = held([P, KP], F32, f"y2_{i}")
-            nc.scalar.copy(out=by_token(y2_sb), in_=product(w2_operand, v_operand, PA, i))
-            y2.append(y2_sb)
+            nc.scalar.copy(out=by_token(y2, i), in_=product(w2_operand, v_operand, PA, i))
 
-        def round_w3(a):
-            grouped = held([P, PACK * H], BF16, f"w3_grouped{a}")
-            round_weight(nc.scalar.copy, w3_raw[a], grouped, 0)
-            return grouped
-
-        for i in range(Y_BANKS):
+        for i in range(Y2_AHEAD):
             second_reading(i)
 
-        w1_q = []
-        grouped = held([P, PACK * H], BF16, "w1_grouped0")
-        round_weight(nc.vector.tensor_copy, w1_raw0, grouped, 0)
-        w1_q.append(quantise_weight(grouped, "w1_0"))
-        grouped = held([P, PACK * H], BF16, "w1_grouped1")
-        for g in range(2):
-            round_weight(nc.vector.tensor_copy, w1_raw1[g], grouped, g * P // 2)
-        w1_q.append(quantise_weight(grouped, "w1_1"))
-
-        hi12, lo12, w3_grouped, w3_q = [], [], [], []
+        hi12 = held([P, NT * KP], F32, "hi12")
+        lo12 = held([P, NT * KP], F32, "lo12")
+        w3_grouped, w3_q = [], []
         for i in range(NT):
             y1 = product(weight_operand(w1_q), v_operand, PA, i)
-            hi = held([P, KP], F32, f"hi12_{i}")
-            lo = held([P, KP], F32, f"lo12_{i}")
-            nc.vector.tensor_tensor(out=by_token(hi), in0=y1, in1=by_token(y2[i]), op=ALU.max)
-            nc.vector.tensor_tensor(out=by_token(lo), in0=y1, in1=by_token(y2[i]), op=ALU.min)
-            hi12.append(hi)
-            lo12.append(lo)
-            if len(y2) < NT:
-                second_reading(len(y2))
-            if i == 1:
-                w3_grouped = [round_w3(a) for a in range(PB)]
-            if i in (2, 4, 6):
+            nc.vector.tensor_tensor(out=by_token(hi12, i), in0=y1, in1=by_token(y2, i), op=ALU.max)
+            nc.vector.tensor_tensor(out=by_token(lo12, i), in0=y1, in1=by_token(y2, i), op=ALU.min)
+            if i + Y2_AHEAD < NT:
+                second_reading(i + Y2_AHEAD)
+            if i in W3_ROUND_AFTER:
+                a = len(w3_grouped)
+                grouped = held([P, PACK * H], BF16, f"w3_grouped{a}")
+                round_weight(nc.scalar.copy, w3_raw[a], grouped, 0)
+                w3_grouped.append(grouped)
+            if i in W3_QUANT_AFTER:
                 a = len(w3_q)
-                w3_q.append(quantise_weight(w3_grouped[a], f"w3_{a}", f"y2_{i}"))
+                w3_q.append(quantise_weight(w3_grouped[a], f"w3_{a}"))
 
         out_rows = out.rearrange("(b p) j -> p b j", p=P)
-        staged = {}
-        for group in STORE_GROUPS:
-            tile = held([P, NB, len(group) * TOK], F32, f"staged{group[0]}")
-            for i in group:
-                staged[i] = (tile, group)
 
-        def extremes(i):
-            y3 = product(weight_operand(w3_q), xs_operand, PB, i)
-            hi = ring.tile([P, KP], F32, name="hi")
-            lo = ring.tile([P, KP], F32, name="lo")
-            nc.vector.tensor_tensor(out=by_token(hi), in0=y3, in1=by_token(hi12[i]), op=ALU.max)
-            nc.vector.tensor_tensor(out=by_token(lo), in0=y3, in1=by_token(lo12[i]), op=ALU.min)
+        def extremes(g):
+            hi = ring.tile([P, 2 * KP], F32, name="hi")
+            lo = ring.tile([P, 2 * KP], F32, name="lo")
+            for u in range(2):
+                i = 2 * g + u
+                y3 = product(weight_operand(w3_q), xs_operand, PB, i)
+                nc.vector.tensor_tensor(out=by_token(hi, u), in0=y3, in1=by_token(hi12, i), op=ALU.max)
+                nc.vector.tensor_tensor(out=by_token(lo, u), in0=y3, in1=by_token(lo12, i), op=ALU.min)
             return hi, lo
 
-        def spread(i, hi, lo):
-            h = ring.tile([P, KP], BF16, name="h", align_bytes=64)
-            engine = nc.gpsimd if i < GPSIMD_TILES else nc.vector
+        def spread(g, hi, lo):
+            h = held([P, 2 * KP], BF16, "h")
+            engine = nc.gpsimd if g < NPAIR - 1 else nc.vector
             engine.tensor_tensor(out=h[:], in0=hi[:], in1=lo[:], op=ALU.subtract)
             return h
 
-        def score(i, h):
-            codes = ring.tile([P, TOK], U32, name="h_codes", align_bytes=64)
-            scales = ring.tile([P, TOK], U8, name="h_scales", align_bytes=64)
-            nc.vector.quantize_mx(out=codes[:].bitcast(FP8X4), scales=scales[:], in_=h[:])
+        def last_product(codes, scales, u):
             bank = opsum.tile([P, NB, TOK], F32, name="obank")
+            cols = slice(u * TOK, (u + 1) * TOK)
             for b in range(NB):
                 nc.tensor.matmul_mx(
                     out=bank[:, b, :], lhsT=w4[:, P * b : P * (b + 1)].bitcast(FP8X4),
-                    lhsT_scale=w4_sc[:, P * b : P * (b + 1)], rhs=codes[:].bitcast(FP8X4), rhs_scale=scales[:],
-                    start=True, stop=True,
+                    lhsT_scale=w4_sc[:, P * b : P * (b + 1)], rhs=codes[:, cols].bitcast(FP8X4),
+                    rhs_scale=scales[:, cols], start=True, stop=True,
                 )
-            tile, group = staged[i]
-            c = (i - group[0]) * TOK
+            return bank
+
+        def scalar_scores(bank, staged):
             for b in range(NB):
                 nc.scalar.activation(
-                    out=tile[:, b, c : c + TOK], in_=bank[:, b, :], func=ACT.Identity, bias=neg_tol[:, b : b + 1]
+                    out=staged[:, b, :], in_=bank[:, b, :], func=ACT.Identity, bias=neg_tol[:, b : b + 1]
                 )
-            if i == group[-1]:
-                nc.sync.dma_start(out=out_rows[:, :, group[0] * TOK : (i + 1) * TOK], in_=tile[:])
 
-        pending = None
-        for i in range(NT):
-            hi, lo = extremes(i)
-            if pending is not None:
-                score(i - 1, pending)
-            pending = spread(i, hi, lo)
-        score(NT - 1, pending)
+        def vector_scores(bank, staged):
+            for b in range(NB):
+                nc.vector.tensor_scalar(
+                    out=staged[:, b, :], in0=bank[:, b, :], scalar1=tol_sb[:, b : b + 1], scalar2=None, op0=ALU.subtract
+                )
+
+        def score(g, h):
+            codes = ring.tile([P, PAIR], U32, name="h_codes", align_bytes=64)
+            scales = ring.tile([P, PAIR], U8, name="h_scales", align_bytes=64)
+            nc.vector.quantize_mx(out=codes[:].bitcast(FP8X4), scales=scales[:], in_=h[:])
+            if g < NPAIR - 1:
+                staged = held([P, NB, PAIR], F32, f"staged{g}")
+                for u in range(2):
+                    scalar_scores(last_product(codes, scales, u), staged[:, :, u * TOK : (u + 1) * TOK])
+                nc.sync.dma_start(out=out_rows[:, :, g * PAIR : (g + 1) * PAIR], in_=staged[:])
+            else:
+                for u, scores in enumerate((scalar_scores, vector_scores)):
+                    staged = held([P, NB, TOK], F32, f"staged_last{u}")
+                    scores(last_product(codes, scales, u), staged[:])
+                    first = g * PAIR + u * TOK
+                    nc.sync.dma_start(out=out_rows[:, :, first : first + TOK], in_=staged[:])
+
+        h = spread(0, *extremes(0))
+        for g in range(1, NPAIR):
+            hi, lo = extremes(g)
+            score(g - 1, h)
+            h = spread(g, hi, lo)
+        score(NPAIR - 1, h)

@@ -126,8 +126,11 @@ def tile_list_dyelot_spread_check_kernel(
 
         def round_weight(copy, raw, grouped, m0):
             width = raw.shape[2] // PACK
-            dst = grouped[:].rearrange("p (t m j) -> p m j t", t=PACK, j=PACK)[:, m0 : m0 + width, :, :]
-            copy(out=dst, in_=raw.rearrange("p j (m t) -> p m j t", t=PACK))
+            dst = grouped[:].rearrange("p (t m j) -> p m t j", t=PACK, j=PACK)[:, m0 : m0 + width, :, :]
+            copy(out=dst, in_=raw.rearrange("p j (m t) -> p m t j", t=PACK))
+
+        def gpsimd_copy(out, in_):
+            nc.gpsimd.tensor_scalar(out=out, in0=in_, scalar1=1.0, scalar2=0.0, op0=ALU.mult, op1=ALU.add)
 
         def quantise_weight(grouped, name):
             codes = held([P, H], U32, name + "_codes")
@@ -231,7 +234,11 @@ def tile_list_dyelot_spread_check_kernel(
             if i in W3_ROUND_AFTER:
                 a = len(w3_grouped)
                 grouped = held([P, PACK * H], BF16, f"w3_grouped{a}")
-                round_weight(nc.scalar.copy, w3_raw[a], grouped, 0)
+                if a == 1:
+                    for c in range(0, H, P):
+                        round_weight(gpsimd_copy, w3_raw[a][:, :, c : c + P], grouped, c // PACK)
+                else:
+                    round_weight(nc.scalar.copy, w3_raw[a], grouped, 0)
                 w3_grouped.append(grouped)
             if i in W3_QUANT_AFTER:
                 a = len(w3_q)

from contextlib import ExitStack

import concourse.mybir as mybir

K, K2, T, S, H, N = 1024, 1536, 4096, 1024, 512, 384
FLOPS = 2 * S * (2 * K * H + K2 * H + H * N)

F32 = mybir.dt.float32
BF16 = mybir.dt.bfloat16
I32 = mybir.dt.int32
U32 = mybir.dt.uint32
U16 = mybir.dt.uint16
U8 = mybir.dt.uint8
FP8X4 = mybir.dt.float8_e4m3fn_x4
FP4X4 = mybir.dt.float4_e2m1fn_x4
ALU = mybir.AluOpType
ACT = mybir.ActivationFunctionType

P = 128
PACK = 4
KP = P * PACK
TOK = 128
NT = S // TOK
PA, PB = K // KP, K2 // KP
NB = N // P
HALF = S // 2
PAIR = 2 * TOK
NPAIR = NT // 2
Y_BANKS = 6
TAB_HEAD = 1024
Y2_AHEAD = 2
W3_ROUND_AFTER = (1, 3, 4)
W3_QUANT_AFTER = (3, 5, 6)


def tile_list_dyelot_spread_check_kernel(
    tc, tab_words, tab_scales, offs, xs_words, xs_scales, w1, w2_words, w2_scales, w3, w4_words, w4_scales, tol, out
):
    nc = tc.nc
    with ExitStack() as ctx:
        keep = ctx.enter_context(tc.tile_pool(name="keep", bufs=1))
        ring = ctx.enter_context(tc.tile_pool(name="ring", bufs=2))
        ypsum = ctx.enter_context(tc.psum_pool(name="ypsum", bufs=Y_BANKS))
        opsum = ctx.enter_context(tc.psum_pool(name="opsum", bufs=2))

        def held(shape, dtype, name, tag=""):
            return keep.tile(shape, dtype, name=name, tag=tag or name, align_bytes=64)

        def load_scale_rows(plane, scales):
            for q in range(4):
                nc.sync.dma_start(
                    out=plane[32 * q : 32 * q + 4, :, :].bitcast(I32),
                    in_=scales[:, 4 * q : 4 * q + 4, :].rearrange("a r c -> r a c").bitcast(I32),
                )

        def load_rows(raw, w, a, c0, c1):
            rows = w[a * KP : (a + 1) * KP, c0:c1]
            nc.sync.dma_start(out=raw, in_=rows.rearrange("(p j) c -> p j c", j=PACK))

        def row_slots(flat):
            return flat.rearrange("p (j c) -> p j c", j=PACK)

        def table_words(a):
            return tab_words[a].rearrange("p t i -> p (t i)").bitcast(I32)

        offsets = keep.tile([P, S // 16], U16, name="offsets")
        nc.sync.dma_start(offsets[:], offs)

        tol_sb = held([P, NB], F32, "tol_sb")
        neg_tol = held([P, NB], F32, "neg_tol")
        with nc.allow_non_contiguous_dma(reason="one tolerance to a partition"):
            nc.scalar.dma_start(out=tol_sb[:], in_=tol.rearrange("(b p) -> p b", p=P))
        nc.scalar.mul(neg_tol[:], tol_sb[:], -1.0)

        tab_sc = held([P, T], U8, "tab_sc")
        nc.vector.memset(tab_sc[:].bitcast(I32), 0)
        w2_sc_raw = held([P, PA, H], U8, "w2_sc_raw")
        v_sc1 = held([P, S], U8, "v_sc1")
        for plane in (w2_sc_raw, v_sc1):
            nc.gpsimd.memset(plane[:].bitcast(I32), 0)

        w2_raw = held([P, PA, 2 * H], U8, "w2_raw")
        nc.sync.dma_start(out=w2_raw[:].bitcast(I32), in_=w2_words.rearrange("a p c -> p a c").bitcast(I32))
        tab0 = held([P, T], I32, "tab0")
        nc.sync.dma_start(out=tab0[:, 0:TAB_HEAD], in_=table_words(0)[:, 0:TAB_HEAD])
        for q in range(4):
            nc.sync.dma_start(
                out=tab_sc[32 * q : 32 * q + 4 * PA, :].bitcast(I32),
                in_=tab_scales[:, 4 * q : 4 * q + 4, :].bitcast(I32),
            )
        nc.sync.dma_start(out=tab0[:, TAB_HEAD:T], in_=table_words(0)[:, TAB_HEAD:T])
        load_scale_rows(w2_sc_raw, w2_scales)
        w1_raw0 = held([P, PACK * H], F32, "w1_raw0")
        load_rows(row_slots(w1_raw0[:]), w1, 0, 0, H)

        w2 = held([P, PA, 2 * H], U8, "w2")
        nc.vector.tensor_copy(
            out=w2[:].bitcast(U16).rearrange("p a (t m) -> p a t m", t=PACK),
            in_=w2_raw[:].bitcast(U16).rearrange("p a (m t) -> p a t m", t=PACK),
        )

        v_sc = held([P, S], U8, "v_sc")
        nc.vector.tensor_copy(v_sc[:], tab_sc[:].indirect(offsets[:]))
        for q in range(4):
            nc.sync.dma_start(
                out=v_sc1[32 * q : 32 * q + 4, :].bitcast(I32),
                in_=v_sc[32 * q + 4 : 32 * q + 8, :].bitcast(I32),
            )
        tab1 = held([P, T], I32, "tab1", "tab_sc")
        nc.sync.dma_start(out=tab1[:], in_=table_words(1))

        v0 = held([P, S], U32, "v0")
        nc.vector.tensor_copy(v0[:], tab0[:].bitcast(U32).indirect(offsets[:]))

        w2_sc = held([P, PA, H], U8, "w2_sc")
        nc.vector.tensor_copy(
            out=w2_sc[:].rearrange("p a (t m) -> p a t m", t=PACK),
            in_=w2_sc_raw[:].rearrange("p a (m t) -> p a t m", t=PACK),
        )
        w1_raw1 = held([P, PACK * H], F32, "w1_raw1", "w2_sc_raw")
        w1_halves = []
        for g in range(2):
            part = row_slots(w1_raw1[:, g * PACK * H // 2 : (g + 1) * PACK * H // 2])
            load_rows(part, w1, 1, g * H // 2, (g + 1) * H // 2)
            w1_halves.append(part)

        def round_weight(copy, raw, grouped, m0):
            width = raw.shape[2] // PACK
            dst = grouped[:].rearrange("p (t m j) -> p m t j", t=PACK, j=PACK)[:, m0 : m0 + width, :, :]
            copy(out=dst, in_=raw.rearrange("p j (m t) -> p m t j", t=PACK))

        def gpsimd_copy(out, in_):
            nc.gpsimd.tensor_scalar(out=out, in0=in_, scalar1=1.0, scalar2=0.0, op0=ALU.mult, op1=ALU.add)

        def quantise_weight(grouped, name):
            codes = held([P, H], U32, name + "_codes")
            scales = held([P, H], U8, name + "_scales")
            nc.vector.quantize_mx(out=codes[:].bitcast(FP8X4), scales=scales[:], in_=grouped[:])
            return codes, scales

        grouped = held([P, PACK * H], BF16, "w1_grouped0")
        round_weight(nc.vector.tensor_copy, row_slots(w1_raw0[:]), grouped, 0)
        w1_q = [quantise_weight(grouped, "w1_0")]

        w3_all = held([P, PB * PACK * H], F32, "w3_raw", "w1_raw0")
        w3_raw = []
        for a in range(PB):
            part = row_slots(w3_all[:, a * PACK * H : (a + 1) * PACK * H])
            load_rows(part, w3, a, 0, H)
            w3_raw.append(part)

        late_sc = held([P, PB * S + N], U8, "late_sc", "w1_grouped0")
        nc.gpsimd.memset(late_sc[:].bitcast(I32), 0)
        xs_sc = late_sc[:, 0 : PB * S].rearrange("p (a c) -> p a c", a=PB)
        w4_sc = late_sc[:, PB * S : PB * S + N]
        load_scale_rows(xs_sc, xs_scales)

        v1 = []
        for g in range(2):
            part = held([P, HALF], U32, f"v1_{g}")
            half_list = offsets[:, g * (HALF // 16) : (g + 1) * (HALF // 16)]
            nc.vector.tensor_copy(part[:], tab1[:].bitcast(U32).indirect(half_list))
            v1.append(part)

        late_words = held([P, PB * S + N], I32, "late_words", "tab_sc")
        xs = []
        for g in range(NPAIR):
            part = late_words[:, g * PB * PAIR : (g + 1) * PB * PAIR].rearrange("p (a c) -> p a c", a=PB)
            cols = xs_words[:, :, g * PAIR : (g + 1) * PAIR, :]
            nc.sync.dma_start(out=part, in_=cols.rearrange("a p c i -> p a (c i)").bitcast(I32))
            xs.append(part)
        w4 = late_words[:, PB * S : PB * S + N]
        nc.sync.dma_start(out=w4, in_=w4_words[0].rearrange("p c i -> p (c i)").bitcast(I32))
        load_scale_rows(w4_sc.rearrange("p (a c) -> p a c", a=1), w4_scales)

        grouped = held([P, PACK * H], BF16, "w1_grouped1")
        round_weight(nc.scalar.copy, w1_halves[0], grouped, 0)
        round_weight(nc.vector.tensor_copy, w1_halves[1], grouped, P // 2)
        w1_q.append(quantise_weight(grouped, "w1_1"))

        def v_operand(a, i):
            cols = slice(i * TOK, (i + 1) * TOK)
            if a == 0:
                return v0[:, cols].bitcast(FP8X4), v_sc[:, cols]
            g, c = divmod(i * TOK, HALF)
            return v1[g][:, c : c + TOK].bitcast(FP8X4), v_sc1[:, cols]

        def xs_operand(a, i):
            g, c = divmod(i * TOK, PAIR)
            return xs[g][:, a, c : c + TOK].bitcast(FP8X4), xs_sc[:, a, i * TOK : (i + 1) * TOK]

        def w2_operand(a, t):
            return w2[:, a, 2 * P * t : 2 * P * (t + 1)].bitcast(FP4X4), w2_sc[:, a, P * t : P * (t + 1)]

        def weight_operand(quantised):
            def operand(a, t):
                codes, scales = quantised[a]
                return codes[:, P * t : P * (t + 1)].bitcast(FP8X4), scales[:, P * t : P * (t + 1)]

            return operand

        def product(weight, moving, passes, i):
            bank = ypsum.tile([P, PACK, TOK], F32, name="ybank")
            for t in range(PACK):
                for a in range(passes):
                    lhsT, lhsT_scale = weight(a, t)
                    rhs, rhs_scale = moving(a, i)
                    nc.tensor.matmul_mx(
                        out=bank[:, t, :], lhsT=lhsT, lhsT_scale=lhsT_scale, rhs=rhs, rhs_scale=rhs_scale,
                        start=(a == 0), stop=(a == passes - 1),
                    )
            return bank[:].rearrange("p t n -> p n t")

        def by_token(flat, i):
            return flat[:, i * KP : (i + 1) * KP].rearrange("p (n t) -> p n t", t=PACK)

        y2 = held([P, NT * KP], F32, "y2", "w2_sc_raw")

        def second_reading(i):
            nc.scalar.copy(out=by_token(y2, i), in_=product(w2_operand, v_operand, PA, i))

        for i in range(Y2_AHEAD):
            second_reading(i)

        hi12 = held([P, NT * KP], F32, "hi12")
        lo12 = held([P, NT * KP], F32, "lo12")
        w3_grouped, w3_q = [], []
        for i in range(NT):
            y1 = product(weight_operand(w1_q), v_operand, PA, i)
            nc.vector.tensor_tensor(out=by_token(hi12, i), in0=y1, in1=by_token(y2, i), op=ALU.max)
            nc.vector.tensor_tensor(out=by_token(lo12, i), in0=y1, in1=by_token(y2, i), op=ALU.min)
            if i + Y2_AHEAD < NT:
                second_reading(i + Y2_AHEAD)
            if i in W3_ROUND_AFTER:
                a = len(w3_grouped)
                grouped = held([P, PACK * H], BF16, f"w3_grouped{a}")
                if a == 1:
                    for c in range(0, H, P):
                        round_weight(gpsimd_copy, w3_raw[a][:, :, c : c + P], grouped, c // PACK)
                else:
                    round_weight(nc.scalar.copy, w3_raw[a], grouped, 0)
                w3_grouped.append(grouped)
            if i in W3_QUANT_AFTER:
                a = len(w3_q)
                w3_q.append(quantise_weight(w3_grouped[a], f"w3_{a}"))

        out_rows = out.rearrange("(b p) j -> p b j", p=P)

        def extremes(g):
            hi = ring.tile([P, 2 * KP], F32, name="hi")
            lo = ring.tile([P, 2 * KP], F32, name="lo")
            for u in range(2):
                i = 2 * g + u
                y3 = product(weight_operand(w3_q), xs_operand, PB, i)
                nc.vector.tensor_tensor(out=by_token(hi, u), in0=y3, in1=by_token(hi12, i), op=ALU.max)
                nc.vector.tensor_tensor(out=by_token(lo, u), in0=y3, in1=by_token(lo12, i), op=ALU.min)
            return hi, lo

        def spread(g, hi, lo):
            h = held([P, 2 * KP], BF16, "h")
            engine = nc.gpsimd if g < NPAIR - 1 else nc.vector
            engine.tensor_tensor(out=h[:], in0=hi[:], in1=lo[:], op=ALU.subtract)
            return h

        def last_product(codes, scales, u):
            bank = opsum.tile([P, NB, TOK], F32, name="obank")
            cols = slice(u * TOK, (u + 1) * TOK)
            for b in range(NB):
                nc.tensor.matmul_mx(
                    out=bank[:, b, :], lhsT=w4[:, P * b : P * (b + 1)].bitcast(FP8X4),
                    lhsT_scale=w4_sc[:, P * b : P * (b + 1)], rhs=codes[:, cols].bitcast(FP8X4),
                    rhs_scale=scales[:, cols], start=True, stop=True,
                )
            return bank

        def scalar_scores(bank, staged):
            for b in range(NB):
                nc.scalar.activation(
                    out=staged[:, b, :], in_=bank[:, b, :], func=ACT.Identity, bias=neg_tol[:, b : b + 1]
                )

        def vector_scores(bank, staged):
            for b in range(NB):
                nc.vector.tensor_scalar(
                    out=staged[:, b, :], in0=bank[:, b, :], scalar1=tol_sb[:, b : b + 1], scalar2=None, op0=ALU.subtract
                )

        def score(g, h):
            codes = ring.tile([P, PAIR], U32, name="h_codes", align_bytes=64)
            scales = ring.tile([P, PAIR], U8, name="h_scales", align_bytes=64)
            nc.vector.quantize_mx(out=codes[:].bitcast(FP8X4), scales=scales[:], in_=h[:])
            if g < NPAIR - 1:
                staged = held([P, NB, PAIR], F32, f"staged{g}")
                for u in range(2):
                    scalar_scores(last_product(codes, scales, u), staged[:, :, u * TOK : (u + 1) * TOK])
                nc.sync.dma_start(out=out_rows[:, :, g * PAIR : (g + 1) * PAIR], in_=staged[:])
            else:
                for u, scores in enumerate((scalar_scores, vector_scores)):
                    staged = held([P, NB, TOK], F32, f"staged_last{u}")
                    scores(last_product(codes, scales, u), staged[:])
                    first = g * PAIR + u * TOK
                    nc.sync.dma_start(out=out_rows[:, :, first : first + TOK], in_=staged[:])

        h = spread(0, *extremes(0))
        for g in range(1, NPAIR):
            hi, lo = extremes(g)
            score(g - 1, h)
            h = spread(g, hi, lo)
        score(NPAIR - 1, h)
